import numpy as np
import ml_dtypes


def mxq(x, axis, fmt="e4m3"):
    dtype, down = {"e4m3": (ml_dtypes.float8_e4m3fn, 7), "e5m2": (ml_dtypes.float8_e5m2, 14)}[fmt]
    v = np.moveaxis(np.asarray(x, np.float32).astype(ml_dtypes.bfloat16).astype(np.float64), axis, -1)
    blocks = v.reshape(v.shape[:-1] + (-1, 32))
    amax = np.abs(blocks).max(-1, keepdims=True)
    byte = np.maximum(np.where(amax > 0, np.frexp(amax)[1] - 1 + 127, 0) - down, 1)
    scale = np.exp2(byte - 127.0)
    codes = (blocks / scale).astype(np.float32).astype(dtype).astype(np.float64)
    return np.moveaxis((codes * scale).reshape(v.shape), -1, axis)


WIDE = False


def mx_kscale(k):
    if not WIDE:
        return np.ones(k)
    levels = np.array([10, -10, 5, -5, 0])
    if k % 512:
        return np.exp2(np.random.permutation(np.resize(levels, k // 32))).repeat(32)
    a = np.empty((k // 512, 16))
    for p in range(k // 512):
        a[p, :8] = np.random.permutation(np.resize(levels, 8))
        for g in range(8):
            far = levels[np.abs(levels - a[p, g]) >= 10]
            a[p, g + 8] = far[np.random.randint(len(far))]
    return np.exp2(a.ravel()).repeat(32)


def f64(x):
    return np.asarray(x).astype(np.float64)


def striped(idx):
    return np.tile(idx.reshape(-1, 16).T, (8, 1)).astype(np.uint16)


def unstriped(offs):
    return offs[:16].T.reshape(-1).astype(np.int64)


def pack_weight(w):
    k, n = w.shape
    w = f64(np.asarray(w, np.float32).astype(ml_dtypes.bfloat16)).reshape(k // 32, 32, n)
    amax = np.abs(w).max(1)
    byte = np.clip(np.where(amax > 0, np.frexp(amax)[1] - 1 + 127 - 7, 1), 1, 254)
    scaled = (w * np.exp2(127.0 - byte)[:, None, :]).reshape(k, n).astype(np.float32)
    words = np.ascontiguousarray(scaled.reshape(k // 512, 128, 4, n).transpose(0, 1, 3, 2)).astype(ml_dtypes.float8_e4m3fn).view(np.uint8)
    return words, np.ascontiguousarray(byte.astype(np.uint8).reshape(k // 512, 16, n))


def unpack_weight(words, scales):
    g, p, n, _ = words.shape
    vals = np.ascontiguousarray(words).view(ml_dtypes.float8_e4m3fn).astype(np.float64) * np.repeat(np.exp2(scales.astype(np.float64) - 127.0), 8, axis=1)[..., None]
    return vals.transpose(0, 1, 3, 2).reshape(g * 512, n)


def relu(v):
    return np.maximum(v, 0.0)


K, T, S, V, N, U = 1024, 2048, 1536, 512, 128, 1024


def setup_inputs():
    n = np.random.standard_normal
    s = mx_kscale(K)[:, None]
    packed_xT = pack_weight(n((K, T)) * s)
    return {
        "x_words": packed_xT[0],
        "x_scales": packed_xT[1],
        "w1": (n((K, N)) / np.sqrt(3 * K) / s).astype(np.float32),
        "w2": (n((K, N)) / np.sqrt(3 * K) / s).astype(np.float32),
        "w3": (n((K, N)) / np.sqrt(3 * K) / s).astype(np.float32),
        "offs": striped(np.random.permutation(T)[:S]),
        "to1": striped(np.random.permutation(U)[:V]),
        "to2": striped(np.random.permutation(U)[:V]),
        "to3": striped(np.random.permutation(U)[:V]),
    }


def reference(x_words, x_scales, w1, w2, w3, offs, to1, to2, to3):
    xq = unpack_weight(x_words, x_scales)[:, unstriped(offs)]
    o0 = np.zeros((N, U))
    o0[:, unstriped(to1)] = mxq(f64(w1), 0, "e4m3").T @ xq[:, :V]
    o1 = np.zeros((N, U))
    o1[:, unstriped(to2)] = mxq(f64(w2), 0, "e4m3").T @ xq[:, V:2 * V]
    o2 = np.zeros((N, U))
    o2[:, unstriped(to3)] = mxq(f64(w3), 0, "e4m3").T @ xq[:, 2 * V:3 * V]
    return relu(o0 + o1 + o2)

@@ -1,0 +1,145 @@
+from contextlib import ExitStack
+
+import concourse.mybir as mybir
+
+K, T, S, V, N, U = 1024, 2048, 1536, 512, 128, 1024
+TAPS = 3
+FLOPS = 2 * K * N * S
+
+F32 = mybir.dt.float32
+BF16 = mybir.dt.bfloat16
+I32 = mybir.dt.int32
+U32 = mybir.dt.uint32
+U16 = mybir.dt.uint16
+U8 = mybir.dt.uint8
+FP8X4 = mybir.dt.float8_e4m3fn_x4
+ADD = mybir.AluOpType.add
+RELU = mybir.ActivationFunctionType.Relu
+
+P = 128
+PACK = 4
+PASSES = K // (P * PACK)
+LIST_ROWS = 16
+OUT_PIECES = (384, 320, 192, 128)
+
+
+def tile_picked_spconv_relu_p_kernel(
+    tc, x_words, x_scales, w1, w2, w3, offs, to1, to2, to3, out
+):
+    nc = tc.nc
+    with ExitStack() as ctx:
+        lists = ctx.enter_context(tc.tile_pool(name="lists", bufs=1))
+        keep = ctx.enter_context(tc.tile_pool(name="keep", bufs=1))
+        psum = ctx.enter_context(tc.psum_pool(name="psum", bufs=1))
+
+        scale_table = keep.tile([P, T], U8, name="scale_table", align_bytes=64)
+        nc.vector.memset(scale_table[:].bitcast(I32), 0)
+        offs_sb = lists.tile([P, S // LIST_ROWS], U16, name="offs_sb")
+        nc.sync.dma_start(offs_sb[:], offs)
+        to_sb = []
+        for d, to in enumerate((to1, to2, to3)):
+            to_tile = lists.tile([P, V // LIST_ROWS], U16, name=f"to_sb{d}")
+            nc.sync.dma_start(to_tile[:], to)
+            to_sb.append(to_tile)
+        nc.sync.dma_start(
+            scale_table[0 : 16 * PASSES, :].bitcast(I32),
+            x_scales.rearrange("z b c -> (z b) c").bitcast(I32),
+        )
+
+        word_table = [keep.tile([P, T], I32, name=f"word_table{z}", align_bytes=64) for z in range(PASSES)]
+        w_raw = [keep.tile([P, PASSES, PACK, N], F32, name=f"w_raw{d}") for d in range(TAPS)]
+
+        def load_words(z):
+            nc.sync.dma_start(word_table[z][:], x_words[z].rearrange("p c r -> p (c r)").bitcast(I32))
+
+        def load_weights(d, w):
+            nc.sync.dma_start(w_raw[d][:], w.rearrange("(z p j) n -> p z j n", z=PASSES, j=PACK))
+
+        load_words(0)
+        load_weights(0, w1)
+        load_weights(1, w2)
+        load_weights(2, w3)
+        load_words(1)
+
+        placed = [keep.tile([P, U], F32, name=f"placed{d}") for d in range(TAPS)]
+        nc.vector.memset(placed[0][:], 0.0)
+        for d in range(1, TAPS):
+            nc.scalar.copy(placed[d][:], placed[0][:])
+
+        x_scale = keep.tile([P, S], U8, name="x_scale", align_bytes=64)
+        nc.vector.memset(x_scale[:].bitcast(I32), 0)
+        picked_scale = keep.tile([P, S], U8, name="picked_scale", align_bytes=64)
+        nc.vector.tensor_copy(picked_scale[:], scale_table[:].indirect(offs_sb[:]))
+        for z in range(PASSES):
+            for q in range(4):
+                nc.sync.dma_start(
+                    x_scale[32 * q + 4 * z : 32 * q + 4 * z + 4, :].bitcast(I32),
+                    picked_scale[16 * z + 4 * q : 16 * z + 4 * q + 4, :].bitcast(I32),
+                )
+        x_code = [keep.tile([P, S], U32, name=f"x_code{z}", align_bytes=64) for z in range(PASSES)]
+
+        def gather_words(z, first, last):
+            nc.vector.tensor_copy(
+                x_code[z][:, first:last],
+                word_table[z][:].bitcast(U32).indirect(offs_sb[:, first // LIST_ROWS : last // LIST_ROWS]),
+            )
+
+        w_code = [keep.tile([P, PASSES * N], U32, name=f"w_code{d}", align_bytes=64) for d in range(TAPS)]
+        w_scale = [keep.tile([P, PASSES * N], U8, name=f"w_scale{d}", align_bytes=64) for d in range(TAPS)]
+
+        def quantize_weights(d):
+            grouped = keep.tile([P, PASSES, N, PACK], BF16, name=f"grouped{d}", align_bytes=64)
+            for z in range(PASSES):
+                nc.scalar.copy(
+                    grouped[:, z].rearrange("p (c i) j -> p c j i", i=4),
+                    w_raw[d][:, z].rearrange("p j (c i) -> p c j i", i=4),
+                )
+            nc.vector.quantize_mx(
+                out=w_code[d][:].bitcast(FP8X4),
+                scales=w_scale[d][:],
+                in_=grouped[:].rearrange("p z n j -> p (z n j)"),
+            )
+
+        y = [keep.tile([P, V], F32, name=f"y{d}") for d in range(TAPS)]
+
+        def multiply(d):
+            acc = psum.tile([P, V], F32, name=f"acc{d}")
+            cols = slice(d * V, (d + 1) * V)
+            for z in range(PASSES):
+                nc.tensor.matmul_mx(
+                    out=acc[:],
+                    lhsT=w_code[d][:, z * N : (z + 1) * N].bitcast(FP8X4),
+                    lhsT_scale=w_scale[d][:, z * N : (z + 1) * N],
+                    rhs=x_code[z][:, cols].bitcast(FP8X4),
+                    rhs_scale=x_scale[4 * z : P, cols],
+                    start=(z == 0),
+                    stop=(z == PASSES - 1),
+                )
+            nc.scalar.copy(y[d][:], acc[:])
+
+        def scatter(d):
+            nc.vector.tensor_copy(placed[d][:].indirect(to_sb[d][:]), y[d][:])
+
+        gather_words(0, 0, S)
+        for d in range(TAPS):
+            quantize_weights(d)
+        gather_words(1, 0, V)
+        multiply(0)
+        gather_words(1, V, S)
+        multiply(1)
+        multiply(2)
+        scatter(0)
+        scatter(1)
+        pair = keep.tile([P, U], F32, name="pair")
+        nc.gpsimd.tensor_tensor(pair[:], placed[0][:], placed[1][:], ADD)
+        scatter(2)
+
+        first = 0
+        for i, width in enumerate(OUT_PIECES):
+            cols = slice(first, first + width)
+            total = keep.tile([P, width], F32, name=f"total{i}")
+            result = keep.tile([P, width], F32, name=f"result{i}")
+            nc.vector.tensor_tensor(total[:], placed[2][:, cols], pair[:, cols], ADD)
+            nc.scalar.activation(result[:], total[:], RELU)
+            nc.sync.dma_start(out[:, cols], result[:])
+            first = first + width

@@ -1,6 +1,7 @@
 from contextlib import ExitStack
 
 import concourse.mybir as mybir
+from concourse.masks import make_identity
 
 K, T, S, V, N, U = 1024, 2048, 1536, 512, 128, 1024
 TAPS = 3
@@ -20,7 +21,8 @@ P = 128
 PACK = 4
 PASSES = K // (P * PACK)
 LIST_ROWS = 16
-OUT_PIECES = (384, 320, 192, 128)
+OUT_PIECES = (384, 256, 256, 128)
+BANK = 512
 
 
 def tile_picked_spconv_relu_p_kernel(
@@ -31,6 +33,7 @@ def tile_picked_spconv_relu_p_kernel(
         lists = ctx.enter_context(tc.tile_pool(name="lists", bufs=1))
         keep = ctx.enter_context(tc.tile_pool(name="keep", bufs=1))
         psum = ctx.enter_context(tc.psum_pool(name="psum", bufs=1))
+        work = ctx.enter_context(tc.psum_pool(name="work", bufs=3))
 
         scale_table = keep.tile([P, T], U8, name="scale_table", align_bytes=64)
         nc.vector.memset(scale_table[:].bitcast(I32), 0)
@@ -66,14 +69,17 @@ def tile_picked_spconv_relu_p_kernel(
         for d in range(1, TAPS):
             nc.scalar.copy(placed[d][:], placed[0][:])
 
-        x_scale = keep.tile([P, S], U8, name="x_scale", align_bytes=64)
-        nc.vector.memset(x_scale[:].bitcast(I32), 0)
+        identity = keep.tile([P, P], F32, name="identity")
+        make_identity(nc, identity[:])
+        x_scale = [keep.tile([P, S], U8, name=f"x_scale{z}", align_bytes=64) for z in range(PASSES)]
+        for z in range(PASSES):
+            nc.vector.memset(x_scale[z][:].bitcast(I32), 0)
         picked_scale = keep.tile([P, S], U8, name="picked_scale", align_bytes=64)
         nc.vector.tensor_copy(picked_scale[:], scale_table[:].indirect(offs_sb[:]))
         for z in range(PASSES):
             for q in range(4):
                 nc.sync.dma_start(
-                    x_scale[32 * q + 4 * z : 32 * q + 4 * z + 4, :].bitcast(I32),
+                    x_scale[z][32 * q : 32 * q + 4, :].bitcast(I32),
                     picked_scale[16 * z + 4 * q : 16 * z + 4 * q + 4, :].bitcast(I32),
                 )
         x_code = [keep.tile([P, S], U32, name=f"x_code{z}", align_bytes=64) for z in range(PASSES)]
@@ -103,7 +109,7 @@ def tile_picked_spconv_relu_p_kernel(
         y = [keep.tile([P, V], F32, name=f"y{d}") for d in range(TAPS)]
 
         def multiply(d):
-            acc = psum.tile([P, V], F32, name=f"acc{d}")
+            acc = work.tile([P, V], F32, name="bank")
             cols = slice(d * V, (d + 1) * V)
             for z in range(PASSES):
                 nc.tensor.matmul_mx(
@@ -111,7 +117,7 @@ def tile_picked_spconv_relu_p_kernel(
                     lhsT=w_code[d][:, z * N : (z + 1) * N].bitcast(FP8X4),
                     lhsT_scale=w_scale[d][:, z * N : (z + 1) * N],
                     rhs=x_code[z][:, cols].bitcast(FP8X4),
-                    rhs_scale=x_scale[4 * z : P, cols],
+                    rhs_scale=x_scale[z][:, cols],
                     start=(z == 0),
                     stop=(z == PASSES - 1),
                 )
@@ -128,18 +134,43 @@ def tile_picked_spconv_relu_p_kernel(
         gather_words(1, V, S)
         multiply(1)
         multiply(2)
+
+        turned = [keep.tile([P, U], F32, name=f"turned{d}") for d in range(2)]
+
+        def turn(d):
+            for first in range(0, U, BANK):
+                bank = work.tile([P, BANK], F32, name="bank")
+                for b in range(0, BANK, P):
+                    nc.tensor.transpose(bank[:, b : b + P], placed[d][:, first + b : first + b + P], identity[:])
+                nc.scalar.copy(turned[d][:, first : first + BANK], bank[:])
+
+        starts = [sum(OUT_PIECES[:i]) for i in range(len(OUT_PIECES))]
+        pair = [psum.tile([P, width], F32, name=f"pair{i}") for i, width in enumerate(OUT_PIECES)]
+
+        def turn_back(i, b, d):
+            block = slice(starts[i] + b, starts[i] + b + P)
+            nc.tensor.matmul(
+                pair[i][:, b : b + P], turned[d][:, block], identity[:],
+                start=(d == 0), stop=(d == 1), is_transpose=True,
+            )
+
         scatter(0)
+        turn(0)
+        for i in range(len(OUT_PIECES)):
+            turn_back(i, 0, 0)
         scatter(1)
-        pair = keep.tile([P, U], F32, name="pair")
-        nc.gpsimd.tensor_tensor(pair[:], placed[0][:], placed[1][:], ADD)
+        turn(1)
+        for i, width in enumerate(OUT_PIECES):
+            turn_back(i, 0, 1)
+            for b in range(P, width, P):
+                turn_back(i, b, 0)
+                turn_back(i, b, 1)
         scatter(2)
 
-        first = 0
         for i, width in enumerate(OUT_PIECES):
-            cols = slice(first, first + width)
+            cols = slice(starts[i], starts[i] + width)
             total = keep.tile([P, width], F32, name=f"total{i}")
             result = keep.tile([P, width], F32, name=f"result{i}")
-            nc.vector.tensor_tensor(total[:], placed[2][:, cols], pair[:, cols], ADD)
+            nc.vector.tensor_tensor(total[:], placed[2][:, cols], pair[i][:], ADD)
             nc.scalar.activation(result[:], total[:], RELU)
             nc.sync.dma_start(out[:, cols], result[:])
-            first = first + width

@@ -21,7 +21,7 @@ P = 128
 PACK = 4
 PASSES = K // (P * PACK)
 LIST_ROWS = 16
-OUT_PIECES = (384, 256, 256, 128)
+OUT_PIECES = (128, 256, 256, 256, 128)
 BANK = 512
 
 
@@ -32,6 +32,7 @@ def tile_picked_spconv_relu_p_kernel(
     with ExitStack() as ctx:
         lists = ctx.enter_context(tc.tile_pool(name="lists", bufs=1))
         keep = ctx.enter_context(tc.tile_pool(name="keep", bufs=1))
+        shared = ctx.enter_context(tc.tile_pool(name="shared", bufs=1))
         psum = ctx.enter_context(tc.psum_pool(name="psum", bufs=1))
         work = ctx.enter_context(tc.psum_pool(name="work", bufs=3))
 
@@ -61,8 +62,8 @@ def tile_picked_spconv_relu_p_kernel(
         load_words(0)
         load_weights(0, w1)
         load_weights(1, w2)
-        load_weights(2, w3)
         load_words(1)
+        load_weights(2, w3)
 
         placed = [keep.tile([P, U], F32, name=f"placed{d}") for d in range(TAPS)]
         nc.vector.memset(placed[0][:], 0.0)
@@ -71,30 +72,32 @@ def tile_picked_spconv_relu_p_kernel(
 
         identity = keep.tile([P, P], F32, name="identity")
         make_identity(nc, identity[:])
-        x_scale = [keep.tile([P, S], U8, name=f"x_scale{z}", align_bytes=64) for z in range(PASSES)]
-        for z in range(PASSES):
-            nc.vector.memset(x_scale[z][:].bitcast(I32), 0)
+        x_scale = keep.tile([P, S], U8, name="x_scale", align_bytes=64)
+        nc.vector.memset(x_scale[:].bitcast(I32), 0)
         picked_scale = keep.tile([P, S], U8, name="picked_scale", align_bytes=64)
         nc.vector.tensor_copy(picked_scale[:], scale_table[:].indirect(offs_sb[:]))
         for z in range(PASSES):
             for q in range(4):
-                nc.sync.dma_start(
-                    x_scale[z][32 * q : 32 * q + 4, :].bitcast(I32),
+                queue = nc.gpsimd if (z, q) == (0, 0) else nc.sync
+                queue.dma_start(
+                    x_scale[32 * q + 4 * z : 32 * q + 4 * z + 4, :].bitcast(I32),
                     picked_scale[16 * z + 4 * q : 16 * z + 4 * q + 4, :].bitcast(I32),
                 )
-        x_code = [keep.tile([P, S], U32, name=f"x_code{z}", align_bytes=64) for z in range(PASSES)]
+        x_code = {}
 
-        def gather_words(z, first, last):
+        def gather_words(z, taps, codes):
+            first, last = taps[0] * V, (taps[-1] + 1) * V
             nc.vector.tensor_copy(
-                x_code[z][:, first:last],
+                codes[:],
                 word_table[z][:].bitcast(U32).indirect(offs_sb[:, first // LIST_ROWS : last // LIST_ROWS]),
             )
+            for d in taps:
+                x_code[z, d] = codes[:, d * V - first : (d + 1) * V - first]
 
         w_code = [keep.tile([P, PASSES * N], U32, name=f"w_code{d}", align_bytes=64) for d in range(TAPS)]
         w_scale = [keep.tile([P, PASSES * N], U8, name=f"w_scale{d}", align_bytes=64) for d in range(TAPS)]
 
-        def quantize_weights(d):
-            grouped = keep.tile([P, PASSES, N, PACK], BF16, name=f"grouped{d}", align_bytes=64)
+        def quantize_weights(d, grouped):
             for z in range(PASSES):
                 nc.scalar.copy(
                     grouped[:, z].rearrange("p (c i) j -> p c j i", i=4),
@@ -106,9 +109,9 @@ def tile_picked_spconv_relu_p_kernel(
                 in_=grouped[:].rearrange("p z n j -> p (z n j)"),
             )
 
-        y = [keep.tile([P, V], F32, name=f"y{d}") for d in range(TAPS)]
+        y = {}
 
-        def multiply(d):
+        def multiply(d, product):
             acc = work.tile([P, V], F32, name="bank")
             cols = slice(d * V, (d + 1) * V)
             for z in range(PASSES):
@@ -116,24 +119,29 @@ def tile_picked_spconv_relu_p_kernel(
                     out=acc[:],
                     lhsT=w_code[d][:, z * N : (z + 1) * N].bitcast(FP8X4),
                     lhsT_scale=w_scale[d][:, z * N : (z + 1) * N],
-                    rhs=x_code[z][:, cols].bitcast(FP8X4),
-                    rhs_scale=x_scale[z][:, cols],
+                    rhs=x_code[z, d].bitcast(FP8X4),
+                    rhs_scale=x_scale[4 * z : P, cols],
                     start=(z == 0),
                     stop=(z == PASSES - 1),
                 )
-            nc.scalar.copy(y[d][:], acc[:])
+            nc.scalar.copy(product, acc[:])
+            y[d] = product
 
         def scatter(d):
-            nc.vector.tensor_copy(placed[d][:].indirect(to_sb[d][:]), y[d][:])
+            nc.vector.tensor_copy(placed[d][:].indirect(to_sb[d][:]), y[d])
 
-        gather_words(0, 0, S)
-        for d in range(TAPS):
-            quantize_weights(d)
-        gather_words(1, 0, V)
-        multiply(0)
-        gather_words(1, V, S)
-        multiply(1)
-        multiply(2)
+        gather_words(0, (0, 1, 2), keep.tile([P, S], U32, name="x_code0", align_bytes=64))
+        for d in range(2):
+            quantize_weights(d, keep.tile([P, PASSES, N, PACK], BF16, name=f"grouped{d}", align_bytes=64))
+        for d in range(2):
+            gather_words(1, (d,), keep.tile([P, V], U32, name=f"x_code1_{d}", align_bytes=64))
+        quantize_weights(2, shared.tile([P, PASSES, N, PACK], BF16, name="grouped2", align_bytes=64, offset=1024))
+        gather_words(1, (2,), shared.tile([P, V], U32, name="x_code1_2", align_bytes=64, offset=0))
+        y_first = shared.tile([P, 2, V], F32, name="y_first", align_bytes=64, offset=2048)
+        y_last = keep.tile([P, V], F32, name="y_last")
+        multiply(0, y_first[:, 0, :])
+        multiply(1, y_first[:, 1, :])
+        multiply(2, y_last[:])
 
         turned = [keep.tile([P, U], F32, name=f"turned{d}") for d in range(2)]
 

@@ -21,8 +21,8 @@ P = 128
 PACK = 4
 PASSES = K // (P * PACK)
 LIST_ROWS = 16
-OUT_PIECES = (128, 256, 256, 256, 128)
-BANK = 512
+OUT_PIECES = (128, 256, 256, 128)
+TURNED = sum(OUT_PIECES)
 
 
 def tile_picked_spconv_relu_p_kernel(
@@ -37,18 +37,13 @@ def tile_picked_spconv_relu_p_kernel(
         work = ctx.enter_context(tc.psum_pool(name="work", bufs=3))
 
         scale_table = keep.tile([P, T], U8, name="scale_table", align_bytes=64)
-        nc.vector.memset(scale_table[:].bitcast(I32), 0)
-        offs_sb = lists.tile([P, S // LIST_ROWS], U16, name="offs_sb")
-        nc.sync.dma_start(offs_sb[:], offs)
-        to_sb = []
-        for d, to in enumerate((to1, to2, to3)):
-            to_tile = lists.tile([P, V // LIST_ROWS], U16, name=f"to_sb{d}")
-            nc.sync.dma_start(to_tile[:], to)
-            to_sb.append(to_tile)
+        nc.vector.memset(scale_table[0:96, :].bitcast(I32), 0)
         nc.sync.dma_start(
-            scale_table[0 : 16 * PASSES, :].bitcast(I32),
+            scale_table[96:P, :].bitcast(I32),
             x_scales.rearrange("z b c -> (z b) c").bitcast(I32),
         )
+        offs_sb = lists.tile([P, S // LIST_ROWS], U16, name="offs_sb")
+        nc.sync.dma_start(offs_sb[:], offs)
 
         word_table = [keep.tile([P, T], I32, name=f"word_table{z}", align_bytes=64) for z in range(PASSES)]
         w_raw = [keep.tile([P, PASSES, PACK, N], F32, name=f"w_raw{d}") for d in range(TAPS)]
@@ -60,12 +55,18 @@ def tile_picked_spconv_relu_p_kernel(
             nc.sync.dma_start(w_raw[d][:], w.rearrange("(z p j) n -> p z j n", z=PASSES, j=PACK))
 
         load_words(0)
+        to_sb = []
+        for d, to in enumerate((to1, to2, to3)):
+            to_tile = lists.tile([P, V // LIST_ROWS], U16, name=f"to_sb{d}")
+            nc.sync.dma_start(to_tile[:], to)
+            to_sb.append(to_tile)
         load_weights(0, w1)
         load_weights(1, w2)
         load_words(1)
         load_weights(2, w3)
 
-        placed = [keep.tile([P, U], F32, name=f"placed{d}") for d in range(TAPS)]
+        placed = [keep.tile([P, U], F32, name=f"placed{d}") for d in range(TAPS - 1)]
+        placed.append(shared.tile([P, U], F32, name="placed_last", align_bytes=64, offset=8192))
         nc.vector.memset(placed[0][:], 0.0)
         for d in range(1, TAPS):
             nc.scalar.copy(placed[d][:], placed[0][:])
@@ -81,7 +82,7 @@ def tile_picked_spconv_relu_p_kernel(
                 queue = nc.gpsimd if (z, q) == (0, 0) else nc.sync
                 queue.dma_start(
                     x_scale[32 * q + 4 * z : 32 * q + 4 * z + 4, :].bitcast(I32),
-                    picked_scale[16 * z + 4 * q : 16 * z + 4 * q + 4, :].bitcast(I32),
+                    picked_scale[96 + 16 * z + 4 * q : 96 + 16 * z + 4 * q + 4, :].bitcast(I32),
                 )
         x_code = {}
 
@@ -143,14 +144,14 @@ def tile_picked_spconv_relu_p_kernel(
         multiply(1, y_first[:, 1, :])
         multiply(2, y_last[:])
 
-        turned = [keep.tile([P, U], F32, name=f"turned{d}") for d in range(2)]
+        turned = [keep.tile([P, TURNED], F32, name=f"turned{d}") for d in range(2)]
 
         def turn(d):
-            for first in range(0, U, BANK):
-                bank = work.tile([P, BANK], F32, name="bank")
-                for b in range(0, BANK, P):
+            for first in range(0, TURNED, TURNED // 2):
+                bank = work.tile([P, V], F32, name="bank")
+                for b in range(0, TURNED // 2, P):
                     nc.tensor.transpose(bank[:, b : b + P], placed[d][:, first + b : first + b + P], identity[:])
-                nc.scalar.copy(turned[d][:, first : first + BANK], bank[:])
+                nc.scalar.copy(turned[d][:, first : first + TURNED // 2], bank[:, 0 : TURNED // 2])
 
         starts = [sum(OUT_PIECES[:i]) for i in range(len(OUT_PIECES))]
         pair = [psum.tile([P, width], F32, name=f"pair{i}") for i, width in enumerate(OUT_PIECES)]
@@ -173,7 +174,12 @@ def tile_picked_spconv_relu_p_kernel(
             for b in range(P, width, P):
                 turn_back(i, b, 0)
                 turn_back(i, b, 1)
+        rest = slice(TURNED, U)
+        pair_rest = keep.tile([P, U - TURNED], F32, name="pair_rest")
+        nc.gpsimd.tensor_tensor(pair_rest[:], placed[0][:, rest], placed[1][:, rest], ADD)
         scatter(2)
+        total_rest = keep.tile([P, U - TURNED], F32, name="total_rest")
+        nc.gpsimd.tensor_tensor(total_rest[:], placed[2][:, rest], pair_rest[:], ADD)
 
         for i, width in enumerate(OUT_PIECES):
             cols = slice(starts[i], starts[i] + width)
@@ -182,3 +188,6 @@ def tile_picked_spconv_relu_p_kernel(
             nc.vector.tensor_tensor(total[:], placed[2][:, cols], pair[i][:], ADD)
             nc.scalar.activation(result[:], total[:], RELU)
             nc.sync.dma_start(out[:, cols], result[:])
+        result_rest = shared.tile([P, U - TURNED], F32, name="result_rest", align_bytes=64, offset=8192)
+        nc.vector.tensor_relu(result_rest[:], total_rest[:])
+        nc.sync.dma_start(out[:, rest], result_rest[:])

@@ -20,9 +20,23 @@ RELU = mybir.ActivationFunctionType.Relu
 P = 128
 PACK = 4
 PASSES = K // (P * PACK)
+QUADRANTS = 4
+QUADRANT = P // QUADRANTS
+QUADRANT_BLOCKS = 4
+PASS_BLOCKS = QUADRANTS * QUADRANT_BLOCKS
 LIST_ROWS = 16
+LINE = 4
+
+SCALE_ROW0 = P - PASSES * PASS_BLOCKS
+GPSIMD_MOVES = 2
 OUT_PIECES = (128, 256, 256, 128)
 TURNED = sum(OUT_PIECES)
+TURN_WIDTH = TURNED // 2
+
+LAST_CODES_AT = 0
+LAST_GROUPED_AT = 1024
+FIRST_PRODUCTS_AT = 2048
+LAST_PLACED_AT = 8192
 
 
 def tile_picked_spconv_relu_p_kernel(
@@ -34,25 +48,30 @@ def tile_picked_spconv_relu_p_kernel(
         keep = ctx.enter_context(tc.tile_pool(name="keep", bufs=1))
         shared = ctx.enter_context(tc.tile_pool(name="shared", bufs=1))
         psum = ctx.enter_context(tc.psum_pool(name="psum", bufs=1))
-        work = ctx.enter_context(tc.psum_pool(name="work", bufs=3))
+        work = ctx.enter_context(tc.psum_pool(name="work", bufs=TAPS))
 
         scale_table = keep.tile([P, T], U8, name="scale_table", align_bytes=64)
-        nc.vector.memset(scale_table[0:96, :].bitcast(I32), 0)
+        nc.vector.memset(scale_table[0:SCALE_ROW0, :].bitcast(I32), 0)
         nc.sync.dma_start(
-            scale_table[96:P, :].bitcast(I32),
+            scale_table[SCALE_ROW0:P, :].bitcast(I32),
             x_scales.rearrange("z b c -> (z b) c").bitcast(I32),
         )
         offs_sb = lists.tile([P, S // LIST_ROWS], U16, name="offs_sb")
         nc.sync.dma_start(offs_sb[:], offs)
 
         word_table = [keep.tile([P, T], I32, name=f"word_table{z}", align_bytes=64) for z in range(PASSES)]
-        w_raw = [keep.tile([P, PASSES, PACK, N], F32, name=f"w_raw{d}") for d in range(TAPS)]
 
         def load_words(z):
             nc.sync.dma_start(word_table[z][:], x_words[z].rearrange("p c r -> p (c r)").bitcast(I32))
 
-        def load_weights(d, w):
-            nc.sync.dma_start(w_raw[d][:], w.rearrange("(z p j) n -> p z j n", z=PASSES, j=PACK))
+        w_raw = {}
+
+        def load_weights(d, w, passes):
+            raw = keep.tile([P, len(passes), PACK, N], F32, name=f"w_raw{d}_{passes[0]}")
+            by_pass = w.rearrange("(z p j) n -> p z j n", z=PASSES, j=PACK)
+            nc.sync.dma_start(raw[:], by_pass[:, passes[0] : passes[-1] + 1])
+            for z in passes:
+                w_raw[d, z] = raw[:, z - passes[0]]
 
         load_words(0)
         to_sb = []
@@ -60,30 +79,35 @@ def tile_picked_spconv_relu_p_kernel(
             to_tile = lists.tile([P, V // LIST_ROWS], U16, name=f"to_sb{d}")
             nc.sync.dma_start(to_tile[:], to)
             to_sb.append(to_tile)
-        load_weights(0, w1)
-        load_weights(1, w2)
+        load_weights(0, w1, (0, 1))
+        load_weights(1, w2, (0, 1))
         load_words(1)
-        load_weights(2, w3)
+        for z in range(PASSES):
+            load_weights(2, w3, (z,))
 
         placed = [keep.tile([P, U], F32, name=f"placed{d}") for d in range(TAPS - 1)]
-        placed.append(shared.tile([P, U], F32, name="placed_last", align_bytes=64, offset=8192))
+        placed.append(shared.tile([P, U], F32, name="placed_last", align_bytes=64, offset=LAST_PLACED_AT))
         nc.vector.memset(placed[0][:], 0.0)
         for d in range(1, TAPS):
             nc.scalar.copy(placed[d][:], placed[0][:])
 
         identity = keep.tile([P, P], F32, name="identity")
         make_identity(nc, identity[:])
+
         x_scale = keep.tile([P, S], U8, name="x_scale", align_bytes=64)
         nc.vector.memset(x_scale[:].bitcast(I32), 0)
         picked_scale = keep.tile([P, S], U8, name="picked_scale", align_bytes=64)
         nc.vector.tensor_copy(picked_scale[:], scale_table[:].indirect(offs_sb[:]))
         for z in range(PASSES):
-            for q in range(4):
-                queue = nc.gpsimd if (z, q) == (0, 0) else nc.sync
+            for q in range(QUADRANTS):
+                queue = nc.gpsimd if z * QUADRANTS + q < GPSIMD_MOVES else nc.sync
+                target = QUADRANT * q + QUADRANT_BLOCKS * z
+                source = SCALE_ROW0 + PASS_BLOCKS * z + QUADRANT_BLOCKS * q
                 queue.dma_start(
-                    x_scale[32 * q + 4 * z : 32 * q + 4 * z + 4, :].bitcast(I32),
-                    picked_scale[96 + 16 * z + 4 * q : 96 + 16 * z + 4 * q + 4, :].bitcast(I32),
+                    x_scale[target : target + QUADRANT_BLOCKS, :].bitcast(I32),
+                    picked_scale[source : source + QUADRANT_BLOCKS, :].bitcast(I32),
                 )
+
         x_code = {}
 
         def gather_words(z, taps, codes):
@@ -101,8 +125,8 @@ def tile_picked_spconv_relu_p_kernel(
         def quantize_weights(d, grouped):
             for z in range(PASSES):
                 nc.scalar.copy(
-                    grouped[:, z].rearrange("p (c i) j -> p c j i", i=4),
-                    w_raw[d][:, z].rearrange("p j (c i) -> p c j i", i=4),
+                    grouped[:, z].rearrange("p (c i) j -> p c j i", i=LINE),
+                    w_raw[d, z].rearrange("p j (c i) -> p c j i", i=LINE),
                 )
             nc.vector.quantize_mx(
                 out=w_code[d][:].bitcast(FP8X4),
@@ -110,48 +134,46 @@ def tile_picked_spconv_relu_p_kernel(
                 in_=grouped[:].rearrange("p z n j -> p (z n j)"),
             )
 
-        y = {}
-
         def multiply(d, product):
             acc = work.tile([P, V], F32, name="bank")
-            cols = slice(d * V, (d + 1) * V)
             for z in range(PASSES):
                 nc.tensor.matmul_mx(
                     out=acc[:],
                     lhsT=w_code[d][:, z * N : (z + 1) * N].bitcast(FP8X4),
                     lhsT_scale=w_scale[d][:, z * N : (z + 1) * N],
                     rhs=x_code[z, d].bitcast(FP8X4),
-                    rhs_scale=x_scale[4 * z : P, cols],
+                    rhs_scale=x_scale[QUADRANT_BLOCKS * z : P, d * V : (d + 1) * V],
                     start=(z == 0),
                     stop=(z == PASSES - 1),
                 )
             nc.scalar.copy(product, acc[:])
-            y[d] = product
+
+        gather_words(0, (0, 1, 2), keep.tile([P, S], U32, name="x_code0", align_bytes=64))
+        for d in range(TAPS - 1):
+            quantize_weights(d, keep.tile([P, PASSES, N, PACK], BF16, name=f"grouped{d}", align_bytes=64))
+        for d in range(TAPS - 1):
+            gather_words(1, (d,), keep.tile([P, V], U32, name=f"x_code1_{d}", align_bytes=64))
+        quantize_weights(
+            2, shared.tile([P, PASSES, N, PACK], BF16, name="grouped2", align_bytes=64, offset=LAST_GROUPED_AT)
+        )
+        gather_words(1, (2,), shared.tile([P, V], U32, name="x_code1_2", align_bytes=64, offset=LAST_CODES_AT))
+        y_first = shared.tile([P, TAPS - 1, V], F32, name="y_first", align_bytes=64, offset=FIRST_PRODUCTS_AT)
+        y_last = keep.tile([P, V], F32, name="y_last")
+        y = [y_first[:, 0, :], y_first[:, 1, :], y_last[:]]
+        for d in range(TAPS):
+            multiply(d, y[d])
 
         def scatter(d):
             nc.vector.tensor_copy(placed[d][:].indirect(to_sb[d][:]), y[d])
 
-        gather_words(0, (0, 1, 2), keep.tile([P, S], U32, name="x_code0", align_bytes=64))
-        for d in range(2):
-            quantize_weights(d, keep.tile([P, PASSES, N, PACK], BF16, name=f"grouped{d}", align_bytes=64))
-        for d in range(2):
-            gather_words(1, (d,), keep.tile([P, V], U32, name=f"x_code1_{d}", align_bytes=64))
-        quantize_weights(2, shared.tile([P, PASSES, N, PACK], BF16, name="grouped2", align_bytes=64, offset=1024))
-        gather_words(1, (2,), shared.tile([P, V], U32, name="x_code1_2", align_bytes=64, offset=0))
-        y_first = shared.tile([P, 2, V], F32, name="y_first", align_bytes=64, offset=2048)
-        y_last = keep.tile([P, V], F32, name="y_last")
-        multiply(0, y_first[:, 0, :])
-        multiply(1, y_first[:, 1, :])
-        multiply(2, y_last[:])
-
-        turned = [keep.tile([P, TURNED], F32, name=f"turned{d}") for d in range(2)]
+        turned = [keep.tile([P, TURNED], F32, name=f"turned{d}") for d in range(TAPS - 1)]
 
         def turn(d):
-            for first in range(0, TURNED, TURNED // 2):
+            for first in range(0, TURNED, TURN_WIDTH):
                 bank = work.tile([P, V], F32, name="bank")
-                for b in range(0, TURNED // 2, P):
+                for b in range(0, TURN_WIDTH, P):
                     nc.tensor.transpose(bank[:, b : b + P], placed[d][:, first + b : first + b + P], identity[:])
-                nc.scalar.copy(turned[d][:, first : first + TURNED // 2], bank[:, 0 : TURNED // 2])
+                nc.scalar.copy(turned[d][:, first : first + TURN_WIDTH], bank[:, 0:TURN_WIDTH])
 
         starts = [sum(OUT_PIECES[:i]) for i in range(len(OUT_PIECES))]
         pair = [psum.tile([P, width], F32, name=f"pair{i}") for i, width in enumerate(OUT_PIECES)]
@@ -178,9 +200,9 @@ def tile_picked_spconv_relu_p_kernel(
         pair_rest = keep.tile([P, U - TURNED], F32, name="pair_rest")
         nc.gpsimd.tensor_tensor(pair_rest[:], placed[0][:, rest], placed[1][:, rest], ADD)
         scatter(2)
+
         total_rest = keep.tile([P, U - TURNED], F32, name="total_rest")
         nc.gpsimd.tensor_tensor(total_rest[:], placed[2][:, rest], pair_rest[:], ADD)
-
         for i, width in enumerate(OUT_PIECES):
             cols = slice(starts[i], starts[i] + width)
             total = keep.tile([P, width], F32, name=f"total{i}")
@@ -188,6 +210,6 @@ def tile_picked_spconv_relu_p_kernel(
             nc.vector.tensor_tensor(total[:], placed[2][:, cols], pair[i][:], ADD)
             nc.scalar.activation(result[:], total[:], RELU)
             nc.sync.dma_start(out[:, cols], result[:])
-        result_rest = shared.tile([P, U - TURNED], F32, name="result_rest", align_bytes=64, offset=8192)
+        result_rest = shared.tile([P, U - TURNED], F32, name="result_rest", align_bytes=64, offset=LAST_PLACED_AT)
         nc.vector.tensor_relu(result_rest[:], total_rest[:])
         nc.sync.dma_start(out[:, rest], result_rest[:])

from contextlib import ExitStack

import concourse.mybir as mybir
from concourse.masks import make_identity

K, T, S, V, N, U = 1024, 2048, 1536, 512, 128, 1024
TAPS = 3
FLOPS = 2 * K * N * S

F32 = mybir.dt.float32
BF16 = mybir.dt.bfloat16
I32 = mybir.dt.int32
U32 = mybir.dt.uint32
U16 = mybir.dt.uint16
U8 = mybir.dt.uint8
FP8X4 = mybir.dt.float8_e4m3fn_x4
ADD = mybir.AluOpType.add
RELU = mybir.ActivationFunctionType.Relu

P = 128
PACK = 4
PASSES = K // (P * PACK)
QUADRANTS = 4
QUADRANT = P // QUADRANTS
QUADRANT_BLOCKS = 4
PASS_BLOCKS = QUADRANTS * QUADRANT_BLOCKS
LIST_ROWS = 16
LINE = 4

SCALE_ROW0 = P - PASSES * PASS_BLOCKS
GPSIMD_MOVES = 2
OUT_PIECES = (128, 256, 256, 128)
TURNED = sum(OUT_PIECES)
TURN_WIDTH = TURNED // 2

LAST_CODES_AT = 0
LAST_GROUPED_AT = 1024
FIRST_PRODUCTS_AT = 2048
LAST_PLACED_AT = 8192


def tile_picked_spconv_relu_p_kernel(
    tc, x_words, x_scales, w1, w2, w3, offs, to1, to2, to3, out
):
    nc = tc.nc
    with ExitStack() as ctx:
        lists = ctx.enter_context(tc.tile_pool(name="lists", bufs=1))
        keep = ctx.enter_context(tc.tile_pool(name="keep", bufs=1))
        shared = ctx.enter_context(tc.tile_pool(name="shared", bufs=1))
        psum = ctx.enter_context(tc.psum_pool(name="psum", bufs=1))
        work = ctx.enter_context(tc.psum_pool(name="work", bufs=TAPS))

        scale_table = keep.tile([P, T], U8, name="scale_table", align_bytes=64)
        nc.vector.memset(scale_table[0:SCALE_ROW0, :].bitcast(I32), 0)
        nc.sync.dma_start(
            scale_table[SCALE_ROW0:P, :].bitcast(I32),
            x_scales.rearrange("z b c -> (z b) c").bitcast(I32),
        )
        offs_sb = lists.tile([P, S // LIST_ROWS], U16, name="offs_sb")
        nc.sync.dma_start(offs_sb[:], offs)

        word_table = [keep.tile([P, T], I32, name=f"word_table{z}", align_bytes=64) for z in range(PASSES)]

        def load_words(z):
            nc.sync.dma_start(word_table[z][:], x_words[z].rearrange("p c r -> p (c r)").bitcast(I32))

        w_raw = {}

        def load_weights(d, w, passes):
            raw = keep.tile([P, len(passes), PACK, N], F32, name=f"w_raw{d}_{passes[0]}")
            by_pass = w.rearrange("(z p j) n -> p z j n", z=PASSES, j=PACK)
            nc.sync.dma_start(raw[:], by_pass[:, passes[0] : passes[-1] + 1])
            for z in passes:
                w_raw[d, z] = raw[:, z - passes[0]]

        load_words(0)
        to_sb = []
        for d, to in enumerate((to1, to2, to3)):
            to_tile = lists.tile([P, V // LIST_ROWS], U16, name=f"to_sb{d}")
            nc.sync.dma_start(to_tile[:], to)
            to_sb.append(to_tile)
        load_weights(0, w1, (0, 1))
        load_weights(1, w2, (0, 1))
        load_words(1)
        for z in range(PASSES):
            load_weights(2, w3, (z,))

        placed = [keep.tile([P, U], F32, name=f"placed{d}") for d in range(TAPS - 1)]
        placed.append(shared.tile([P, U], F32, name="placed_last", align_bytes=64, offset=LAST_PLACED_AT))
        nc.vector.memset(placed[0][:], 0.0)
        for d in range(1, TAPS):
            nc.scalar.copy(placed[d][:], placed[0][:])

        identity = keep.tile([P, P], F32, name="identity")
        make_identity(nc, identity[:])

        x_scale = keep.tile([P, S], U8, name="x_scale", align_bytes=64)
        nc.vector.memset(x_scale[:].bitcast(I32), 0)
        picked_scale = keep.tile([P, S], U8, name="picked_scale", align_bytes=64)
        nc.vector.tensor_copy(picked_scale[:], scale_table[:].indirect(offs_sb[:]))
        for z in range(PASSES):
            for q in range(QUADRANTS):
                queue = nc.gpsimd if z * QUADRANTS + q < GPSIMD_MOVES else nc.sync
                target = QUADRANT * q + QUADRANT_BLOCKS * z
                source = SCALE_ROW0 + PASS_BLOCKS * z + QUADRANT_BLOCKS * q
                queue.dma_start(
                    x_scale[target : target + QUADRANT_BLOCKS, :].bitcast(I32),
                    picked_scale[source : source + QUADRANT_BLOCKS, :].bitcast(I32),
                )

        x_code = {}

        def gather_words(z, taps, codes):
            first, last = taps[0] * V, (taps[-1] + 1) * V
            nc.vector.tensor_copy(
                codes[:],
                word_table[z][:].bitcast(U32).indirect(offs_sb[:, first // LIST_ROWS : last // LIST_ROWS]),
            )
            for d in taps:
                x_code[z, d] = codes[:, d * V - first : (d + 1) * V - first]

        w_code = [keep.tile([P, PASSES * N], U32, name=f"w_code{d}", align_bytes=64) for d in range(TAPS)]
        w_scale = [keep.tile([P, PASSES * N], U8, name=f"w_scale{d}", align_bytes=64) for d in range(TAPS)]

        def quantize_weights(d, grouped):
            for z in range(PASSES):
                nc.scalar.copy(
                    grouped[:, z].rearrange("p (c i) j -> p c j i", i=LINE),
                    w_raw[d, z].rearrange("p j (c i) -> p c j i", i=LINE),
                )
            nc.vector.quantize_mx(
                out=w_code[d][:].bitcast(FP8X4),
                scales=w_scale[d][:],
                in_=grouped[:].rearrange("p z n j -> p (z n j)"),
            )

        def multiply(d, product):
            acc = work.tile([P, V], F32, name="bank")
            for z in range(PASSES):
                nc.tensor.matmul_mx(
                    out=acc[:],
                    lhsT=w_code[d][:, z * N : (z + 1) * N].bitcast(FP8X4),
                    lhsT_scale=w_scale[d][:, z * N : (z + 1) * N],
                    rhs=x_code[z, d].bitcast(FP8X4),
                    rhs_scale=x_scale[QUADRANT_BLOCKS * z : P, d * V : (d + 1) * V],
                    start=(z == 0),
                    stop=(z == PASSES - 1),
                )
            nc.scalar.copy(product, acc[:])

        gather_words(0, (0, 1, 2), keep.tile([P, S], U32, name="x_code0", align_bytes=64))
        for d in range(TAPS - 1):
            quantize_weights(d, keep.tile([P, PASSES, N, PACK], BF16, name=f"grouped{d}", align_bytes=64))
        for d in range(TAPS - 1):
            gather_words(1, (d,), keep.tile([P, V], U32, name=f"x_code1_{d}", align_bytes=64))
        quantize_weights(
            2, shared.tile([P, PASSES, N, PACK], BF16, name="grouped2", align_bytes=64, offset=LAST_GROUPED_AT)
        )
        gather_words(1, (2,), shared.tile([P, V], U32, name="x_code1_2", align_bytes=64, offset=LAST_CODES_AT))
        y_first = shared.tile([P, TAPS - 1, V], F32, name="y_first", align_bytes=64, offset=FIRST_PRODUCTS_AT)
        y_last = keep.tile([P, V], F32, name="y_last")
        y = [y_first[:, 0, :], y_first[:, 1, :], y_last[:]]
        for d in range(TAPS):
            multiply(d, y[d])

        def scatter(d):
            nc.vector.tensor_copy(placed[d][:].indirect(to_sb[d][:]), y[d])

        turned = [keep.tile([P, TURNED], F32, name=f"turned{d}") for d in range(TAPS - 1)]

        def turn(d):
            for first in range(0, TURNED, TURN_WIDTH):
                bank = work.tile([P, V], F32, name="bank")
                for b in range(0, TURN_WIDTH, P):
                    nc.tensor.transpose(bank[:, b : b + P], placed[d][:, first + b : first + b + P], identity[:])
                nc.scalar.copy(turned[d][:, first : first + TURN_WIDTH], bank[:, 0:TURN_WIDTH])

        starts = [sum(OUT_PIECES[:i]) for i in range(len(OUT_PIECES))]
        pair = [psum.tile([P, width], F32, name=f"pair{i}") for i, width in enumerate(OUT_PIECES)]

        def turn_back(i, b, d):
            block = slice(starts[i] + b, starts[i] + b + P)
            nc.tensor.matmul(
                pair[i][:, b : b + P], turned[d][:, block], identity[:],
                start=(d == 0), stop=(d == 1), is_transpose=True,
            )

        scatter(0)
        turn(0)
        for i in range(len(OUT_PIECES)):
            turn_back(i, 0, 0)
        scatter(1)
        turn(1)
        for i, width in enumerate(OUT_PIECES):
            turn_back(i, 0, 1)
            for b in range(P, width, P):
                turn_back(i, b, 0)
                turn_back(i, b, 1)
        rest = slice(TURNED, U)
        pair_rest = keep.tile([P, U - TURNED], F32, name="pair_rest")
        nc.gpsimd.tensor_tensor(pair_rest[:], placed[0][:, rest], placed[1][:, rest], ADD)
        scatter(2)

        total_rest = keep.tile([P, U - TURNED], F32, name="total_rest")
        nc.gpsimd.tensor_tensor(total_rest[:], placed[2][:, rest], pair_rest[:], ADD)
        for i, width in enumerate(OUT_PIECES):
            cols = slice(starts[i], starts[i] + width)
            total = keep.tile([P, width], F32, name=f"total{i}")
            result = keep.tile([P, width], F32, name=f"result{i}")
            nc.vector.tensor_tensor(total[:], placed[2][:, cols], pair[i][:], ADD)
            nc.scalar.activation(result[:], total[:], RELU)
            nc.sync.dma_start(out[:, cols], result[:])
        result_rest = shared.tile([P, U - TURNED], F32, name="result_rest", align_bytes=64, offset=LAST_PLACED_AT)
        nc.vector.tensor_relu(result_rest[:], total_rest[:])
        nc.sync.dma_start(out[:, rest], result_rest[:])
